import numpy as np
import ml_dtypes


def mxq(x, axis, fmt="e4m3"):
    dtype, down = {"e4m3": (ml_dtypes.float8_e4m3fn, 7), "e5m2": (ml_dtypes.float8_e5m2, 14)}[fmt]
    v = np.moveaxis(np.asarray(x, np.float32).astype(ml_dtypes.bfloat16).astype(np.float64), axis, -1)
    blocks = v.reshape(v.shape[:-1] + (-1, 32))
    amax = np.abs(blocks).max(-1, keepdims=True)
    byte = np.maximum(np.where(amax > 0, np.frexp(amax)[1] - 1 + 127, 0) - down, 1)
    scale = np.exp2(byte - 127.0)
    codes = (blocks / scale).astype(np.float32).astype(dtype).astype(np.float64)
    return np.moveaxis((codes * scale).reshape(v.shape), -1, axis)


WIDE = False


def mx_kscale(k):
    if not WIDE:
        return np.ones(k)
    levels = np.array([10, -10, 5, -5, 0])
    if k % 512:
        return np.exp2(np.random.permutation(np.resize(levels, k // 32))).repeat(32)
    a = np.empty((k // 512, 16))
    for p in range(k // 512):
        a[p, :8] = np.random.permutation(np.resize(levels, 8))
        for g in range(8):
            far = levels[np.abs(levels - a[p, g]) >= 10]
            a[p, g + 8] = far[np.random.randint(len(far))]
    return np.exp2(a.ravel()).repeat(32)


def f64(x):
    return np.asarray(x).astype(np.float64)


def striped(idx):
    return np.tile(idx.reshape(-1, 16).T, (8, 1)).astype(np.uint16)


def unstriped(offs):
    return offs[:16].T.reshape(-1).astype(np.int64)


def pack_weight(w):
    k, n = w.shape
    w = f64(np.asarray(w, np.float32).astype(ml_dtypes.bfloat16)).reshape(k // 32, 32, n)
    amax = np.abs(w).max(1)
    byte = np.clip(np.where(amax > 0, np.frexp(amax)[1] - 1 + 127 - 7, 1), 1, 254)
    scaled = (w * np.exp2(127.0 - byte)[:, None, :]).reshape(k, n).astype(np.float32)
    words = np.ascontiguousarray(scaled.reshape(k // 512, 128, 4, n).transpose(0, 1, 3, 2)).astype(ml_dtypes.float8_e4m3fn).view(np.uint8)
    return words, np.ascontiguousarray(byte.astype(np.uint8).reshape(k // 512, 16, n))


def unpack_weight(words, scales):
    g, p, n, _ = words.shape
    vals = np.ascontiguousarray(words).view(ml_dtypes.float8_e4m3fn).astype(np.float64) * np.repeat(np.exp2(scales.astype(np.float64) - 127.0), 8, axis=1)[..., None]
    return vals.transpose(0, 1, 3, 2).reshape(g * 512, n)


def sigmoid(v):
    return 1.0 / (1.0 + np.exp(-np.maximum(v, -700.0)))


K, T, S, V = 512, 1024, 512, 256


def setup_inputs():
    n = np.random.standard_normal
    s = mx_kscale(K)[:, None]
    packed_xT = pack_weight(n((K, T)) * s)
    return {
        "x_words": packed_xT[0],
        "x_scales": packed_xT[1],
        "hT": (n((K, V)) / np.sqrt(K) / s).astype(np.float32),
        "gT": (n((K, V)) / np.sqrt(K) / s).astype(np.float32),
        "fT": (n((K, V)) / np.sqrt(K) / s).astype(np.float32),
        "offs": striped(np.random.permutation(T)[:S]),
    }


def reference(x_words, x_scales, hT, gT, fT, offs):
    hTq = mxq(f64(hT), 0, "e4m3")
    xq = unpack_weight(x_words, x_scales)[:, unstriped(offs)]
    y = hTq.T @ xq
    e0 = np.exp(y)
    s0 = np.log(e0.sum(axis=1, keepdims=True))
    l0 = y - s0
    fTq = mxq(f64(fT), 0, "e4m3")
    ss = fTq.T @ xq
    e2 = np.exp(ss)
    s2 = np.log(e2.sum(axis=1, keepdims=True))
    l2 = ss - s2
    gTq = mxq(f64(gT), 0, "e4m3")
    z = gTq.T @ xq
    e1 = np.exp(z)
    s1 = np.log(e1.sum(axis=1, keepdims=True))
    l1 = z - s1
    p0 = np.exp(l0)
    p1 = np.exp(l1)
    m1 = np.log(0.5 * (p0 + p1))
    t1 = p0 * (l0 - m1) + p1 * (l1 - m1)
    j1 = t1.sum(axis=1, keepdims=True)
    p2 = np.exp(l2)
    m2 = np.log(0.5 * (p0 + p2))
    t2 = p0 * (l0 - m2) + p2 * (l2 - m2)
    j2 = t2.sum(axis=1, keepdims=True)
    ww = sigmoid(4.0 * (j1 - j2))
    gg = l0 - (l2 + (l1 - l2) * ww)
    ex = np.exp(gg - gg.max(axis=1, keepdims=True))
    return ex / ex.sum(axis=1, keepdims=True)

@@ -1,0 +1,212 @@
+from contextlib import ExitStack
+
+import concourse.mybir as mybir
+
+K, T, S, V = 512, 1024, 512, 256
+FLOPS = 3 * 2 * K * V * S
+
+F32 = mybir.dt.float32
+BF16 = mybir.dt.bfloat16
+I32 = mybir.dt.int32
+U32 = mybir.dt.uint32
+U16 = mybir.dt.uint16
+U8 = mybir.dt.uint8
+FP8X4 = mybir.dt.float8_e4m3fn_x4
+ALU = mybir.AluOpType
+ACT = mybir.ActivationFunctionType
+AX = mybir.AxisListType
+
+P = 128
+PACK = 4
+TILES = V // P
+LAST, EARLY, MIDDLE = 0, 1, 2
+LOG_FLOOR = 2.0 ** -60
+
+
+def tile_picked_ydola_soft_p_kernel(tc, x_words, x_scales, hT, gT, fT, offs, out):
+    nc = tc.nc
+    with ExitStack() as ctx:
+        keep = ctx.enter_context(tc.tile_pool(name="keep", bufs=1))
+        psum = ctx.enter_context(tc.psum_pool(name="psum", bufs=1))
+
+        def wide(name):
+            return keep.tile([P, S], F32, name=name)
+
+        def stat(name, cols):
+            return keep.tile([P, cols], F32, name=name)
+
+        offsets = keep.tile([P, S // 16], U16, name="offsets")
+        nc.sync.dma_start(offsets[:], offs)
+        table_words = keep.tile([P, T], I32, name="table_words")
+        nc.sync.dma_start(out=table_words[:], in_=x_words[0].rearrange("p n t -> p (n t)").bitcast(I32))
+        table_scales = keep.tile([P, T], U8, name="table_scales")
+        nc.gpsimd.memset(table_scales[:].bitcast(I32), 0)
+        for q in range(4):
+            nc.sync.dma_start(
+                out=table_scales[32 * q : 32 * q + 4, :].bitcast(I32),
+                in_=x_scales[0][4 * q : 4 * q + 4, :].bitcast(I32),
+            )
+        raw = []
+        for m, states in enumerate((hT, gT, fT)):
+            raw.append(keep.tile([P, PACK, V], F32, name="raw%d" % m))
+            nc.sync.dma_start(out=raw[m][:], in_=states.rearrange("(p j) w -> p j w", j=PACK))
+
+        floor = stat("floor", 1)
+        nc.gpsimd.memset(floor[:], LOG_FLOOR)
+
+        x_codes = keep.tile([P, S], U32, name="x_codes", align_bytes=64)
+        nc.vector.tensor_copy(x_codes[:], table_words[:].bitcast(U32).indirect(offsets[:]))
+        x_sc = keep.tile([P, S], U8, name="x_sc", align_bytes=64)
+        nc.vector.tensor_copy(x_sc[:], table_scales[:].indirect(offsets[:]))
+
+        neg_max = stat("neg_max", 3 * TILES)
+        sums = stat("sums", 3 * TILES)
+        col = lambda m, t: slice(m * TILES + t, m * TILES + t + 1)
+        pair = lambda m, t: slice((m - 1) * TILES + t, (m - 1) * TILES + t + 1)
+        logits, e, neg_last = {}, {}, {}
+
+        def cast(m, t):
+            grouped = keep.tile([P, P, PACK], BF16, name="grouped%d%d" % (m, t), align_bytes=64)
+            src = raw[m][:, :, t * P : (t + 1) * P].rearrange("p j w -> p w j")
+            if m == MIDDLE:
+                nc.gpsimd.tensor_scalar(grouped[:], src, 1.0, 0.0, ALU.mult, ALU.add)
+            elif (m, t) == (LAST, 1):
+                nc.vector.tensor_copy(grouped[:], src)
+            else:
+                nc.scalar.activation(grouped[:], src, ACT.Copy)
+            return grouped
+
+        def product(m, t, grouped):
+            codes = keep.tile([P, P], U32, name="codes%d%d" % (m, t), align_bytes=64)
+            scales = keep.tile([P, P], U8, name="scales%d%d" % (m, t), align_bytes=64)
+            nc.vector.quantize_mx(
+                out=codes[:].bitcast(FP8X4), scales=scales[:], in_=grouped[:].rearrange("p w j -> p (w j)")
+            )
+            logits[m, t] = psum.tile([P, S], F32, name="logits%d%d" % (m, t))
+            nc.tensor.matmul_mx(
+                out=logits[m, t][:],
+                lhsT=codes[:].bitcast(FP8X4),
+                lhsT_scale=scales[:],
+                rhs=x_codes[:].bitcast(FP8X4),
+                rhs_scale=x_sc[:],
+                start=True,
+                stop=True,
+            )
+
+        def exponentials(m, t):
+            if m == LAST:
+                neg_last[t] = wide("neg_last%d" % t)
+                nc.vector.tensor_scalar(
+                    neg_last[t][:], logits[m, t][:], -1.0, None, ALU.mult, ALU.min, accum_out=neg_max[:, col(m, t)]
+                )
+            else:
+                nc.vector.tensor_reduce(neg_max[:, col(m, t)], logits[m, t][:], AX.X, ALU.max, negate=True)
+            e[m, t] = wide("e%d%d" % (m, t))
+            nc.scalar.activation(
+                e[m, t][:], logits[m, t][:], ACT.Exp, bias=neg_max[:, col(m, t)], accum_out=sums[:, col(m, t)]
+            )
+
+        own = stat("own", 2 * TILES)
+        mixed = stat("mixed", 2 * TILES)
+        ratio = stat("ratio", 2 * TILES)
+        inv_last = stat("inv_last", TILES)
+        inv = stat("inv", 2 * TILES)
+        q, log_q = {}, {}
+
+        def own_term(m, t):
+            nc.vector.scalar_tensor_tensor(
+                wide("own_terms%d%d" % (m, t))[:], logits[m, t][:], neg_max[:, col(m, t)], e[m, t][:],
+                ALU.add, ALU.mult, accum_out=own[:, pair(m, t)],
+            )
+
+        def ratios(m):
+            nc.vector.tensor_tensor(
+                ratio[:, (m - 1) * TILES : m * TILES], sums[:, m * TILES : (m + 1) * TILES], inv_last[:], ALU.mult
+            )
+
+        def mixture(m, t):
+            q[m, t] = wide("q%d%d" % (m, t))
+            nc.vector.scalar_tensor_tensor(
+                q[m, t][:], e[LAST, t][:], ratio[:, pair(m, t)], e[m, t][:], ALU.mult, ALU.add
+            )
+
+        def log_mixture(m, t):
+            log_q[m, t] = wide("log_q%d%d" % (m, t))
+            nc.scalar.activation(log_q[m, t][:], q[m, t][:], ACT.Ln, bias=floor[:], scale=inv[:, pair(m, t)])
+
+        def mixed_term(m, t):
+            nc.vector.scalar_tensor_tensor(
+                wide("mixed_terms%d%d" % (m, t))[:], q[m, t][:], inv[:, pair(m, t)], log_q[m, t][:],
+                ALU.mult, ALU.mult, accum_out=mixed[:, pair(m, t)],
+            )
+
+        for m in (LAST, EARLY, MIDDLE):
+            grouped = [cast(m, t) for t in range(TILES)]
+            for t in range(TILES):
+                product(m, t, grouped[t])
+            for t in range(TILES):
+                exponentials(m, t)
+        nc.vector.reciprocal(inv_last[:], sums[:, 0:TILES])
+        ratios(EARLY)
+        for t in range(TILES):
+            own_term(EARLY, t)
+        mixture(EARLY, 0)
+        nc.vector.reciprocal(inv[:], sums[:, TILES:])
+        ratios(MIDDLE)
+        mixture(EARLY, 1)
+        for t in range(TILES):
+            mixture(MIDDLE, t)
+        log_sums = stat("log_sums", 2 * TILES)
+        nc.scalar.activation(log_sums[:], sums[:, TILES:], ACT.Ln)
+        for t in range(TILES):
+            for m in (EARLY, MIDDLE):
+                log_mixture(m, t)
+        for t in range(TILES):
+            own_term(MIDDLE, t)
+
+        own_mean = stat("own_mean", 2 * TILES)
+        nc.vector.scalar_tensor_tensor(own_mean[:], own[:], 2.0, inv[:], ALU.mult, ALU.mult)
+        mixed_term(EARLY, 0)
+        entropy = stat("entropy", 2 * TILES)
+        nc.vector.scalar_tensor_tensor(entropy[:], log_sums[:], 2.0, own_mean[:], ALU.mult, ALU.subtract)
+        mixed_term(MIDDLE, 0)
+        entropy_gap = stat("entropy_gap", TILES)
+        nc.vector.tensor_tensor(entropy_gap[:], entropy[:, TILES:], entropy[:, 0:TILES], ALU.subtract)
+        for m in (EARLY, MIDDLE):
+            mixed_term(m, 1)
+
+        weight = {}
+        for t in range(TILES):
+            partial = stat("partial%d" % t, 1)
+            nc.scalar.activation(
+                partial[:], mixed[:, pair(EARLY, t)], ACT.Identity, bias=entropy_gap[:, t : t + 1], scale=-2.0
+            )
+            lean = stat("lean%d" % t, 1)
+            nc.scalar.activation(lean[:], mixed[:, pair(MIDDLE, t)], ACT.Tanh, bias=partial[:], scale=2.0)
+            for m, sign in ((EARLY, 0.5), (MIDDLE, -0.5)):
+                weight[m, t] = stat("weight%d%d" % (m, t), 1)
+                nc.scalar.activation(weight[m, t][:], lean[:], ACT.Copy, bias=0.5, scale=sign)
+
+        half, neg_g = {}, {}
+        for t in range(TILES):
+            half[t] = wide("half%d" % t)
+            nc.vector.scalar_tensor_tensor(
+                half[t][:], logits[EARLY, t][:], weight[EARLY, t][:], neg_last[t][:], ALU.mult, ALU.add
+            )
+        for t in range(TILES):
+            neg_g[t] = wide("neg_g%d" % t)
+            nc.vector.scalar_tensor_tensor(
+                neg_g[t][:], logits[MIDDLE, t][:], weight[MIDDLE, t][:], half[t][:], ALU.mult, ALU.add
+            )
+        final = {}
+        for t in range(TILES):
+            low = stat("low%d" % t, 1)
+            nc.vector.tensor_reduce(low[:], neg_g[t][:], AX.X, ALU.min)
+            final[t] = (wide("final%d" % t), stat("total%d" % t, 1))
+            nc.scalar.activation(final[t][0][:], neg_g[t][:], ACT.Exp, bias=low[:], scale=-1.0, accum_out=final[t][1][:])
+        for t in range(TILES):
+            inv_total = stat("inv_total%d" % t, 1)
+            nc.vector.reciprocal(inv_total[:], final[t][1][:])
+            result = wide("result%d" % t)
+            nc.vector.tensor_scalar(result[:], final[t][0][:], inv_total[:], None, ALU.mult)
+            nc.sync.dma_start(out=out[t * P : (t + 1) * P, :], in_=result[:])

@@ -20,6 +20,8 @@ P = 128
 PACK = 4
 TILES = V // P
 LAST, EARLY, MIDDLE = 0, 1, 2
+LAYERS = (LAST, EARLY, MIDDLE)
+PAIRS = [(m, t) for t in range(TILES) for m in (EARLY, MIDDLE)]
 LOG_FLOOR = 2.0 ** -60
 
 
@@ -59,151 +61,122 @@ def tile_picked_ydola_soft_p_kernel(tc, x_words, x_scales, hT, gT, fT, offs, out
         x_sc = keep.tile([P, S], U8, name="x_sc", align_bytes=64)
         nc.vector.tensor_copy(x_sc[:], table_scales[:].indirect(offsets[:]))
 
+        logits = {}
+        for m in LAYERS:
+            grouped = []
+            for t in range(TILES):
+                grouped.append(keep.tile([P, P, PACK], BF16, name="grouped%d%d" % (m, t), align_bytes=64))
+                src = raw[m][:, :, t * P : (t + 1) * P].rearrange("p j w -> p w j")
+                if (m, t) in ((EARLY, 0),):
+                    nc.vector.tensor_copy(grouped[t][:], src)
+                else:
+                    nc.scalar.activation(grouped[t][:], src, ACT.Copy)
+            for t in range(TILES):
+                codes = keep.tile([P, P], U32, name="codes%d%d" % (m, t), align_bytes=64)
+                scales = keep.tile([P, P], U8, name="scales%d%d" % (m, t), align_bytes=64)
+                nc.vector.quantize_mx(
+                    out=codes[:].bitcast(FP8X4), scales=scales[:], in_=grouped[t][:].rearrange("p w j -> p (w j)")
+                )
+                logits[m, t] = psum.tile([P, S], F32, name="logits%d%d" % (m, t))
+                nc.tensor.matmul_mx(
+                    out=logits[m, t][:],
+                    lhsT=codes[:].bitcast(FP8X4),
+                    lhsT_scale=scales[:],
+                    rhs=x_codes[:].bitcast(FP8X4),
+                    rhs_scale=x_sc[:],
+                    start=True,
+                    stop=True,
+                )
+
         neg_max = stat("neg_max", 3 * TILES)
         sums = stat("sums", 3 * TILES)
         col = lambda m, t: slice(m * TILES + t, m * TILES + t + 1)
         pair = lambda m, t: slice((m - 1) * TILES + t, (m - 1) * TILES + t + 1)
-        logits, e, neg_last = {}, {}, {}
-
-        def cast(m, t):
-            grouped = keep.tile([P, P, PACK], BF16, name="grouped%d%d" % (m, t), align_bytes=64)
-            src = raw[m][:, :, t * P : (t + 1) * P].rearrange("p j w -> p w j")
-            if m == MIDDLE:
-                nc.gpsimd.tensor_scalar(grouped[:], src, 1.0, 0.0, ALU.mult, ALU.add)
-            elif (m, t) == (LAST, 1):
-                nc.vector.tensor_copy(grouped[:], src)
-            else:
-                nc.scalar.activation(grouped[:], src, ACT.Copy)
-            return grouped
-
-        def product(m, t, grouped):
-            codes = keep.tile([P, P], U32, name="codes%d%d" % (m, t), align_bytes=64)
-            scales = keep.tile([P, P], U8, name="scales%d%d" % (m, t), align_bytes=64)
-            nc.vector.quantize_mx(
-                out=codes[:].bitcast(FP8X4), scales=scales[:], in_=grouped[:].rearrange("p w j -> p (w j)")
-            )
-            logits[m, t] = psum.tile([P, S], F32, name="logits%d%d" % (m, t))
-            nc.tensor.matmul_mx(
-                out=logits[m, t][:],
-                lhsT=codes[:].bitcast(FP8X4),
-                lhsT_scale=scales[:],
-                rhs=x_codes[:].bitcast(FP8X4),
-                rhs_scale=x_sc[:],
-                start=True,
-                stop=True,
-            )
-
-        def exponentials(m, t):
-            if m == LAST:
-                neg_last[t] = wide("neg_last%d" % t)
+        e, neg, lead = {}, {}, {}
+        for m in LAYERS:
+            for t in range(TILES):
+                neg[m, t] = wide("neg%d%d" % (m, t))
                 nc.vector.tensor_scalar(
-                    neg_last[t][:], logits[m, t][:], -1.0, None, ALU.mult, ALU.min, accum_out=neg_max[:, col(m, t)]
+                    neg[m, t][:], logits[m, t][:], -1.0, None, ALU.mult, ALU.min, accum_out=neg_max[:, col(m, t)]
                 )
-            else:
-                nc.vector.tensor_reduce(neg_max[:, col(m, t)], logits[m, t][:], AX.X, ALU.max, negate=True)
-            e[m, t] = wide("e%d%d" % (m, t))
-            nc.scalar.activation(
-                e[m, t][:], logits[m, t][:], ACT.Exp, bias=neg_max[:, col(m, t)], accum_out=sums[:, col(m, t)]
-            )
+                e[m, t] = wide("e%d%d" % (m, t))
+                nc.scalar.activation(
+                    e[m, t][:], logits[m, t][:], ACT.Exp, bias=neg_max[:, col(m, t)], accum_out=sums[:, col(m, t)]
+                )
+                if m != LAST:
+                    lead[m, t] = wide("lead%d%d" % (m, t))
+                    nc.gpsimd.tensor_tensor(lead[m, t][:], neg[LAST, t][:], neg[m, t][:], ALU.subtract)
 
         own = stat("own", 2 * TILES)
         mixed = stat("mixed", 2 * TILES)
         ratio = stat("ratio", 2 * TILES)
         inv_last = stat("inv_last", TILES)
         inv = stat("inv", 2 * TILES)
+
+        nc.vector.reciprocal(inv_last[:], sums[:, 0:TILES])
+        for m in (EARLY, MIDDLE):
+            for t in range(TILES):
+                if (m, t) == (MIDDLE, TILES - 1):
+                    nc.vector.tensor_tensor(
+                        ratio[:].rearrange("p (m t) -> p m t", t=TILES),
+                        sums[:, TILES:].rearrange("p (m t) -> p m t", t=TILES),
+                        inv_last[:].unsqueeze(1).to_broadcast([P, 2, TILES]),
+                        ALU.mult,
+                    )
+                    nc.vector.reciprocal(inv[:], sums[:, TILES:])
+                nc.vector.scalar_tensor_tensor(
+                    wide("own_terms%d%d" % (m, t))[:], logits[m, t][:], neg_max[:, col(m, t)], e[m, t][:],
+                    ALU.add, ALU.mult, accum_out=own[:, pair(m, t)],
+                )
         q, log_q = {}, {}
-
-        def own_term(m, t):
-            nc.vector.scalar_tensor_tensor(
-                wide("own_terms%d%d" % (m, t))[:], logits[m, t][:], neg_max[:, col(m, t)], e[m, t][:],
-                ALU.add, ALU.mult, accum_out=own[:, pair(m, t)],
-            )
-
-        def ratios(m):
-            nc.vector.tensor_tensor(
-                ratio[:, (m - 1) * TILES : m * TILES], sums[:, m * TILES : (m + 1) * TILES], inv_last[:], ALU.mult
-            )
-
-        def mixture(m, t):
+        for m, t in PAIRS:
             q[m, t] = wide("q%d%d" % (m, t))
             nc.vector.scalar_tensor_tensor(
                 q[m, t][:], e[LAST, t][:], ratio[:, pair(m, t)], e[m, t][:], ALU.mult, ALU.add
             )
-
-        def log_mixture(m, t):
+        log_sums = stat("log_sums", 2 * TILES)
+        nc.scalar.activation(log_sums[:], sums[:, TILES:], ACT.Ln)
+        for m, t in PAIRS:
             log_q[m, t] = wide("log_q%d%d" % (m, t))
             nc.scalar.activation(log_q[m, t][:], q[m, t][:], ACT.Ln, bias=floor[:], scale=inv[:, pair(m, t)])
 
-        def mixed_term(m, t):
-            nc.vector.scalar_tensor_tensor(
-                wide("mixed_terms%d%d" % (m, t))[:], q[m, t][:], inv[:, pair(m, t)], log_q[m, t][:],
-                ALU.mult, ALU.mult, accum_out=mixed[:, pair(m, t)],
-            )
-
-        for m in (LAST, EARLY, MIDDLE):
-            grouped = [cast(m, t) for t in range(TILES)]
-            for t in range(TILES):
-                product(m, t, grouped[t])
-            for t in range(TILES):
-                exponentials(m, t)
-        nc.vector.reciprocal(inv_last[:], sums[:, 0:TILES])
-        ratios(EARLY)
-        for t in range(TILES):
-            own_term(EARLY, t)
-        mixture(EARLY, 0)
-        nc.vector.reciprocal(inv[:], sums[:, TILES:])
-        ratios(MIDDLE)
-        mixture(EARLY, 1)
-        for t in range(TILES):
-            mixture(MIDDLE, t)
-        log_sums = stat("log_sums", 2 * TILES)
-        nc.scalar.activation(log_sums[:], sums[:, TILES:], ACT.Ln)
-        for t in range(TILES):
-            for m in (EARLY, MIDDLE):
-                log_mixture(m, t)
-        for t in range(TILES):
-            own_term(MIDDLE, t)
-
         own_mean = stat("own_mean", 2 * TILES)
-        nc.vector.scalar_tensor_tensor(own_mean[:], own[:], 2.0, inv[:], ALU.mult, ALU.mult)
-        mixed_term(EARLY, 0)
+        nc.vector.tensor_tensor(own_mean[:], own[:], inv[:], ALU.mult)
         entropy = stat("entropy", 2 * TILES)
-        nc.vector.scalar_tensor_tensor(entropy[:], log_sums[:], 2.0, own_mean[:], ALU.mult, ALU.subtract)
-        mixed_term(MIDDLE, 0)
+        nc.vector.tensor_tensor(entropy[:], log_sums[:], own_mean[:], ALU.subtract)
         entropy_gap = stat("entropy_gap", TILES)
         nc.vector.tensor_tensor(entropy_gap[:], entropy[:, TILES:], entropy[:, 0:TILES], ALU.subtract)
-        for m in (EARLY, MIDDLE):
-            mixed_term(m, 1)
 
-        weight = {}
+        odds, share = {}, {}
         for t in range(TILES):
+            for m in (EARLY, MIDDLE):
+                nc.vector.scalar_tensor_tensor(
+                    wide("mixed_terms%d%d" % (m, t))[:], q[m, t][:], inv[:, pair(m, t)], log_q[m, t][:],
+                    ALU.mult, ALU.mult, accum_out=mixed[:, pair(m, t)],
+                )
             partial = stat("partial%d" % t, 1)
-            nc.scalar.activation(
-                partial[:], mixed[:, pair(EARLY, t)], ACT.Identity, bias=entropy_gap[:, t : t + 1], scale=-2.0
+            nc.vector.tensor_scalar(
+                partial[:], mixed[:, pair(EARLY, t)], entropy_gap[:, t : t + 1], -4.0, ALU.subtract, ALU.mult
             )
-            lean = stat("lean%d" % t, 1)
-            nc.scalar.activation(lean[:], mixed[:, pair(MIDDLE, t)], ACT.Tanh, bias=partial[:], scale=2.0)
-            for m, sign in ((EARLY, 0.5), (MIDDLE, -0.5)):
-                weight[m, t] = stat("weight%d%d" % (m, t), 1)
-                nc.scalar.activation(weight[m, t][:], lean[:], ACT.Copy, bias=0.5, scale=sign)
+            odds[t] = stat("odds%d" % t, 1)
+            nc.scalar.activation(odds[t][:], mixed[:, pair(MIDDLE, t)], ACT.Exp, bias=partial[:], scale=4.0)
+            share[t] = stat("share%d" % t, 2)
+            nc.scalar.activation(share[t][:, 0:1], odds[t][:], ACT.Copy, bias=1.0)
 
-        half, neg_g = {}, {}
+        blend = {}
         for t in range(TILES):
-            half[t] = wide("half%d" % t)
+            blend[t] = wide("blend%d" % t)
             nc.vector.scalar_tensor_tensor(
-                half[t][:], logits[EARLY, t][:], weight[EARLY, t][:], neg_last[t][:], ALU.mult, ALU.add
+                blend[t][:], lead[EARLY, t][:], odds[t][:], lead[MIDDLE, t][:], ALU.mult, ALU.add
             )
-        for t in range(TILES):
-            neg_g[t] = wide("neg_g%d" % t)
-            nc.vector.scalar_tensor_tensor(
-                neg_g[t][:], logits[MIDDLE, t][:], weight[MIDDLE, t][:], half[t][:], ALU.mult, ALU.add
-            )
+            nc.vector.reciprocal(share[t][:, 1:2], share[t][:, 0:1])
         final = {}
         for t in range(TILES):
             low = stat("low%d" % t, 1)
-            nc.vector.tensor_reduce(low[:], neg_g[t][:], AX.X, ALU.min)
+            neg_g = wide("neg_g%d" % t)
+            nc.vector.tensor_scalar(neg_g[:], blend[t][:], share[t][:, 1:2], None, ALU.mult, ALU.min, accum_out=low[:])
             final[t] = (wide("final%d" % t), stat("total%d" % t, 1))
-            nc.scalar.activation(final[t][0][:], neg_g[t][:], ACT.Exp, bias=low[:], scale=-1.0, accum_out=final[t][1][:])
+            nc.scalar.activation(final[t][0][:], neg_g[:], ACT.Exp, bias=low[:], scale=-1.0, accum_out=final[t][1][:])
         for t in range(TILES):
             inv_total = stat("inv_total%d" % t, 1)
             nc.vector.reciprocal(inv_total[:], final[t][1][:])

@@ -22,7 +22,7 @@ TILES = V // P
 LAST, EARLY, MIDDLE = 0, 1, 2
 LAYERS = (LAST, EARLY, MIDDLE)
 PAIRS = [(m, t) for t in range(TILES) for m in (EARLY, MIDDLE)]
-LOG_FLOOR = 2.0 ** -60
+LOG_OF_FLOOR = -42.0
 
 
 def tile_picked_ydola_soft_p_kernel(tc, x_words, x_scales, hT, gT, fT, offs, out):
@@ -31,8 +31,8 @@ def tile_picked_ydola_soft_p_kernel(tc, x_words, x_scales, hT, gT, fT, offs, out
         keep = ctx.enter_context(tc.tile_pool(name="keep", bufs=1))
         psum = ctx.enter_context(tc.psum_pool(name="psum", bufs=1))
 
-        def wide(name):
-            return keep.tile([P, S], F32, name=name)
+        def wide(name, tag=None):
+            return keep.tile([P, S], F32, name=name, tag=tag or name, align_bytes=64)
 
         def stat(name, cols):
             return keep.tile([P, cols], F32, name=name)
@@ -50,11 +50,13 @@ def tile_picked_ydola_soft_p_kernel(tc, x_words, x_scales, hT, gT, fT, offs, out
             )
         raw = []
         for m, states in enumerate((hT, gT, fT)):
-            raw.append(keep.tile([P, PACK, V], F32, name="raw%d" % m))
+            raw.append(keep.tile([P, PACK, V], F32, name="raw%d" % m, tag="raw%d" % m, align_bytes=64))
             nc.sync.dma_start(out=raw[m][:], in_=states.rearrange("(p j) w -> p j w", j=PACK))
 
+        floor_log = stat("floor_log", 1)
+        nc.gpsimd.memset(floor_log[:], LOG_OF_FLOOR)
         floor = stat("floor", 1)
-        nc.gpsimd.memset(floor[:], LOG_FLOOR)
+        nc.scalar.activation(floor[:], floor_log[:], ACT.Exp)
 
         x_codes = keep.tile([P, S], U32, name="x_codes", align_bytes=64)
         nc.vector.tensor_copy(x_codes[:], table_words[:].bitcast(U32).indirect(offsets[:]))
@@ -65,12 +67,13 @@ def tile_picked_ydola_soft_p_kernel(tc, x_words, x_scales, hT, gT, fT, offs, out
         for m in LAYERS:
             grouped = []
             for t in range(TILES):
-                grouped.append(keep.tile([P, P, PACK], BF16, name="grouped%d%d" % (m, t), align_bytes=64))
-                src = raw[m][:, :, t * P : (t + 1) * P].rearrange("p j w -> p w j")
+                grouped.append(keep.tile([P, P, PACK], BF16, name="grouped%d%d" % (m, t), tag="grouped%d%d" % (m, t), align_bytes=64))
+                src = raw[m][:, :, t * P : (t + 1) * P].rearrange("p j (c i) -> p c j i", i=PACK)
+                dst = grouped[t][:].rearrange("p (c i) j -> p c j i", i=PACK)
                 if (m, t) in ((EARLY, 0),):
-                    nc.vector.tensor_copy(grouped[t][:], src)
+                    nc.vector.tensor_copy(dst, src)
                 else:
-                    nc.scalar.activation(grouped[t][:], src, ACT.Copy)
+                    nc.scalar.activation(dst, src, ACT.Copy)
             for t in range(TILES):
                 codes = keep.tile([P, P], U32, name="codes%d%d" % (m, t), align_bytes=64)
                 scales = keep.tile([P, P], U8, name="scales%d%d" % (m, t), align_bytes=64)
@@ -95,11 +98,11 @@ def tile_picked_ydola_soft_p_kernel(tc, x_words, x_scales, hT, gT, fT, offs, out
         e, neg, lead = {}, {}, {}
         for m in LAYERS:
             for t in range(TILES):
-                neg[m, t] = wide("neg%d%d" % (m, t))
+                neg[m, t] = wide("neg%d%d" % (m, t), {(EARLY, 0): "grouped20", (EARLY, 1): "grouped21"}.get((m, t)))
                 nc.vector.tensor_scalar(
                     neg[m, t][:], logits[m, t][:], -1.0, None, ALU.mult, ALU.min, accum_out=neg_max[:, col(m, t)]
                 )
-                e[m, t] = wide("e%d%d" % (m, t))
+                e[m, t] = wide("e%d%d" % (m, t), "raw%d" % MIDDLE if (m, t) == (LAST, 0) else None)
                 nc.scalar.activation(
                     e[m, t][:], logits[m, t][:], ACT.Exp, bias=neg_max[:, col(m, t)], accum_out=sums[:, col(m, t)]
                 )
@@ -117,12 +120,10 @@ def tile_picked_ydola_soft_p_kernel(tc, x_words, x_scales, hT, gT, fT, offs, out
         for m in (EARLY, MIDDLE):
             for t in range(TILES):
                 if (m, t) == (MIDDLE, TILES - 1):
-                    nc.vector.tensor_tensor(
-                        ratio[:].rearrange("p (m t) -> p m t", t=TILES),
-                        sums[:, TILES:].rearrange("p (m t) -> p m t", t=TILES),
-                        inv_last[:].unsqueeze(1).to_broadcast([P, 2, TILES]),
-                        ALU.mult,
-                    )
+                    for u in range(TILES):
+                        nc.scalar.activation(
+                            ratio[:, u :: TILES], sums[:, TILES + u :: TILES], ACT.Identity, scale=inv_last[:, u : u + 1]
+                        )
                     nc.vector.reciprocal(inv[:], sums[:, TILES:])
                 nc.vector.scalar_tensor_tensor(
                     wide("own_terms%d%d" % (m, t))[:], logits[m, t][:], neg_max[:, col(m, t)], e[m, t][:],
@@ -180,6 +181,7 @@ def tile_picked_ydola_soft_p_kernel(tc, x_words, x_scales, hT, gT, fT, offs, out
         for t in range(TILES):
             inv_total = stat("inv_total%d" % t, 1)
             nc.vector.reciprocal(inv_total[:], final[t][1][:])
-            result = wide("result%d" % t)
-            nc.vector.tensor_scalar(result[:], final[t][0][:], inv_total[:], None, ALU.mult)
-            nc.sync.dma_start(out=out[t * P : (t + 1) * P, :], in_=result[:])
+            for c in range(0, S, S // 2):
+                result = keep.tile([P, S // 2], F32, name="result%d_%d" % (t, c))
+                nc.vector.tensor_scalar(result[:], final[t][0][:, c : c + S // 2], inv_total[:], None, ALU.mult)
+                nc.sync.dma_start(out=out[t * P : (t + 1) * P, c : c + S // 2], in_=result[:])

@@ -18,11 +18,19 @@ AX = mybir.AxisListType
 
 P = 128
 PACK = 4
+QUADRANTS = 4
 TILES = V // P
 LAST, EARLY, MIDDLE = 0, 1, 2
 LAYERS = (LAST, EARLY, MIDDLE)
-PAIRS = [(m, t) for t in range(TILES) for m in (EARLY, MIDDLE)]
+EARLIER = (EARLY, MIDDLE)
+PAIRS = [(m, t) for t in range(TILES) for m in EARLIER]
+FINAL_PRODUCT = (MIDDLE, TILES - 1)
+SHARPNESS = 4.0
 LOG_OF_FLOOR = -42.0
+MIXED_EARLY = 0
+LOG_SUM = {EARLY: 1, MIDDLE: 2}
+OWN = {EARLY: 3, MIDDLE: 4}
+TERMS = 5
 
 
 def tile_picked_ydola_soft_p_kernel(tc, x_words, x_scales, hT, gT, fT, offs, out):
@@ -31,8 +39,8 @@ def tile_picked_ydola_soft_p_kernel(tc, x_words, x_scales, hT, gT, fT, offs, out
         keep = ctx.enter_context(tc.tile_pool(name="keep", bufs=1))
         psum = ctx.enter_context(tc.psum_pool(name="psum", bufs=1))
 
-        def wide(name, tag=None):
-            return keep.tile([P, S], F32, name=name, tag=tag or name, align_bytes=64)
+        def wide(name, reuse=None):
+            return keep.tile([P, S], F32, name=name, tag=reuse or name, align_bytes=64)
 
         def stat(name, cols):
             return keep.tile([P, cols], F32, name=name)
@@ -43,10 +51,10 @@ def tile_picked_ydola_soft_p_kernel(tc, x_words, x_scales, hT, gT, fT, offs, out
         nc.sync.dma_start(out=table_words[:], in_=x_words[0].rearrange("p n t -> p (n t)").bitcast(I32))
         table_scales = keep.tile([P, T], U8, name="table_scales")
         nc.gpsimd.memset(table_scales[:].bitcast(I32), 0)
-        for q in range(4):
+        for quad in range(QUADRANTS):
             nc.sync.dma_start(
-                out=table_scales[32 * q : 32 * q + 4, :].bitcast(I32),
-                in_=x_scales[0][4 * q : 4 * q + 4, :].bitcast(I32),
+                out=table_scales[32 * quad : 32 * quad + 4, :].bitcast(I32),
+                in_=x_scales[0][4 * quad : 4 * quad + 4, :].bitcast(I32),
             )
         raw = []
         for m, states in enumerate((hT, gT, fT)):
@@ -67,10 +75,11 @@ def tile_picked_ydola_soft_p_kernel(tc, x_words, x_scales, hT, gT, fT, offs, out
         for m in LAYERS:
             grouped = []
             for t in range(TILES):
-                grouped.append(keep.tile([P, P, PACK], BF16, name="grouped%d%d" % (m, t), tag="grouped%d%d" % (m, t), align_bytes=64))
+                name = "grouped%d%d" % (m, t)
+                grouped.append(keep.tile([P, P, PACK], BF16, name=name, tag=name, align_bytes=64))
                 src = raw[m][:, :, t * P : (t + 1) * P].rearrange("p j (c i) -> p c j i", i=PACK)
                 dst = grouped[t][:].rearrange("p (c i) j -> p c j i", i=PACK)
-                if (m, t) in ((EARLY, 0),):
+                if (m, t) == (EARLY, 0):
                     nc.vector.tensor_copy(dst, src)
                 else:
                     nc.scalar.activation(dst, src, ACT.Copy)
@@ -91,76 +100,94 @@ def tile_picked_ydola_soft_p_kernel(tc, x_words, x_scales, hT, gT, fT, offs, out
                     stop=True,
                 )
 
-        neg_max = stat("neg_max", 3 * TILES)
-        sums = stat("sums", 3 * TILES)
-        col = lambda m, t: slice(m * TILES + t, m * TILES + t + 1)
-        pair = lambda m, t: slice((m - 1) * TILES + t, (m - 1) * TILES + t + 1)
+        def col(m, t):
+            return slice(m * TILES + t, m * TILES + t + 1)
+
+        def pair(m, t):
+            return col(m - 1, t)
+
+        neg_max = stat("neg_max", len(LAYERS) * TILES)
+        sums = stat("sums", len(LAYERS) * TILES)
         e, neg, lead = {}, {}, {}
         for m in LAYERS:
             for t in range(TILES):
-                neg[m, t] = wide("neg%d%d" % (m, t), {(EARLY, 0): "grouped20", (EARLY, 1): "grouped21"}.get((m, t)))
-                nc.vector.tensor_scalar(
-                    neg[m, t][:], logits[m, t][:], -1.0, None, ALU.mult, ALU.min, accum_out=neg_max[:, col(m, t)]
-                )
+                if (m, t) == FINAL_PRODUCT:
+                    nc.vector.tensor_reduce(neg_max[:, col(m, t)], logits[m, t][:], AX.X, ALU.max, negate=True)
+                else:
+                    neg[m, t] = wide("neg%d%d" % (m, t), "grouped%d%d" % (MIDDLE, t) if m == EARLY else None)
+                    nc.vector.tensor_scalar(
+                        neg[m, t][:], logits[m, t][:], -1.0, None, ALU.mult, ALU.min, accum_out=neg_max[:, col(m, t)]
+                    )
                 e[m, t] = wide("e%d%d" % (m, t), "raw%d" % MIDDLE if (m, t) == (LAST, 0) else None)
                 nc.scalar.activation(
                     e[m, t][:], logits[m, t][:], ACT.Exp, bias=neg_max[:, col(m, t)], accum_out=sums[:, col(m, t)]
                 )
                 if m != LAST:
                     lead[m, t] = wide("lead%d%d" % (m, t))
-                    nc.gpsimd.tensor_tensor(lead[m, t][:], neg[LAST, t][:], neg[m, t][:], ALU.subtract)
+                    if (m, t) == FINAL_PRODUCT:
+                        nc.vector.tensor_tensor(lead[m, t][:], logits[m, t][:], neg[LAST, t][:], ALU.add)
+                    else:
+                        nc.gpsimd.tensor_tensor(lead[m, t][:], neg[LAST, t][:], neg[m, t][:], ALU.subtract)
 
-        own = stat("own", 2 * TILES)
-        mixed = stat("mixed", 2 * TILES)
-        ratio = stat("ratio", 2 * TILES)
+        terms = keep.tile([P, TILES, TERMS], F32, name="terms")
+        coef = keep.tile([P, TILES, TERMS], F32, name="coef")
+        nc.gpsimd.memset(coef[:, :, MIXED_EARLY : LOG_SUM[EARLY] + 1], -SHARPNESS)
+        nc.gpsimd.memset(coef[:, :, LOG_SUM[MIDDLE] : LOG_SUM[MIDDLE] + 1], SHARPNESS)
+        mixed_middle = stat("mixed_middle", TILES)
+        ratio = stat("ratio", len(EARLIER) * TILES)
         inv_last = stat("inv_last", TILES)
-        inv = stat("inv", 2 * TILES)
+        inv = stat("inv", len(EARLIER) * TILES)
+
+        def own_term(m, t, reuse=None):
+            nc.vector.scalar_tensor_tensor(
+                wide("own_terms%d%d" % (m, t), reuse)[:], logits[m, t][:], neg_max[:, col(m, t)], e[m, t][:],
+                ALU.add, ALU.mult, accum_out=terms[:, t, OWN[m] : OWN[m] + 1],
+            )
 
         nc.vector.reciprocal(inv_last[:], sums[:, 0:TILES])
-        for m in (EARLY, MIDDLE):
+        for m in EARLIER:
             for t in range(TILES):
-                if (m, t) == (MIDDLE, TILES - 1):
-                    for u in range(TILES):
-                        nc.scalar.activation(
-                            ratio[:, u :: TILES], sums[:, TILES + u :: TILES], ACT.Identity, scale=inv_last[:, u : u + 1]
-                        )
-                    nc.vector.reciprocal(inv[:], sums[:, TILES:])
-                nc.vector.scalar_tensor_tensor(
-                    wide("own_terms%d%d" % (m, t))[:], logits[m, t][:], neg_max[:, col(m, t)], e[m, t][:],
-                    ALU.add, ALU.mult, accum_out=own[:, pair(m, t)],
-                )
-        q, log_q = {}, {}
-        for m, t in PAIRS:
-            q[m, t] = wide("q%d%d" % (m, t))
-            nc.vector.scalar_tensor_tensor(
-                q[m, t][:], e[LAST, t][:], ratio[:, pair(m, t)], e[m, t][:], ALU.mult, ALU.add
+                if (m, t) != FINAL_PRODUCT:
+                    own_term(m, t)
+        for t in range(TILES):
+            nc.scalar.activation(
+                ratio[:, t::TILES], sums[:, TILES + t :: TILES], ACT.Identity, scale=inv_last[:, t : t + 1]
             )
-        log_sums = stat("log_sums", 2 * TILES)
-        nc.scalar.activation(log_sums[:], sums[:, TILES:], ACT.Ln)
+        nc.vector.reciprocal(inv[:], sums[:, TILES:])
+
+        scaled_q, log_q = {}, {}
+        for m, t in PAIRS:
+            scaled_q[m, t] = wide("scaled_q%d%d" % (m, t))
+            nc.vector.scalar_tensor_tensor(
+                scaled_q[m, t][:], e[LAST, t][:], ratio[:, pair(m, t)], e[m, t][:], ALU.mult, ALU.add
+            )
+        own_term(MIDDLE, TILES - 1, "e%d%d" % (LAST, TILES - 1))
+
+        nc.scalar.activation(
+            terms[:, :, LOG_SUM[EARLY] : LOG_SUM[MIDDLE] + 1].rearrange("p t m -> p m t"),
+            sums[:, TILES:].rearrange("p (m t) -> p m t", t=TILES),
+            ACT.Ln,
+        )
+        for m, factor in ((EARLY, SHARPNESS), (MIDDLE, -SHARPNESS)):
+            nc.scalar.activation(coef[:, :, OWN[m]], inv[:, (m - 1) * TILES : m * TILES], ACT.Copy, scale=factor)
         for m, t in PAIRS:
             log_q[m, t] = wide("log_q%d%d" % (m, t))
-            nc.scalar.activation(log_q[m, t][:], q[m, t][:], ACT.Ln, bias=floor[:], scale=inv[:, pair(m, t)])
-
-        own_mean = stat("own_mean", 2 * TILES)
-        nc.vector.tensor_tensor(own_mean[:], own[:], inv[:], ALU.mult)
-        entropy = stat("entropy", 2 * TILES)
-        nc.vector.tensor_tensor(entropy[:], log_sums[:], own_mean[:], ALU.subtract)
-        entropy_gap = stat("entropy_gap", TILES)
-        nc.vector.tensor_tensor(entropy_gap[:], entropy[:, TILES:], entropy[:, 0:TILES], ALU.subtract)
+            nc.scalar.activation(log_q[m, t][:], scaled_q[m, t][:], ACT.Ln, bias=floor[:], scale=inv[:, pair(m, t)])
 
         odds, share = {}, {}
         for t in range(TILES):
-            for m in (EARLY, MIDDLE):
+            for m, mixed in ((EARLY, terms[:, t, MIXED_EARLY : MIXED_EARLY + 1]), (MIDDLE, mixed_middle[:, t : t + 1])):
                 nc.vector.scalar_tensor_tensor(
-                    wide("mixed_terms%d%d" % (m, t))[:], q[m, t][:], inv[:, pair(m, t)], log_q[m, t][:],
-                    ALU.mult, ALU.mult, accum_out=mixed[:, pair(m, t)],
+                    wide("mixed_terms%d%d" % (m, t))[:], scaled_q[m, t][:], inv[:, pair(m, t)], log_q[m, t][:],
+                    ALU.mult, ALU.mult, accum_out=mixed,
                 )
             partial = stat("partial%d" % t, 1)
-            nc.vector.tensor_scalar(
-                partial[:], mixed[:, pair(EARLY, t)], entropy_gap[:, t : t + 1], -4.0, ALU.subtract, ALU.mult
+            nc.vector.scalar_tensor_tensor(
+                stat("weighted%d" % t, TERMS)[:], terms[:, t, :], 1.0, coef[:, t, :],
+                ALU.mult, ALU.mult, accum_out=partial[:],
             )
             odds[t] = stat("odds%d" % t, 1)
-            nc.scalar.activation(odds[t][:], mixed[:, pair(MIDDLE, t)], ACT.Exp, bias=partial[:], scale=4.0)
+            nc.scalar.activation(odds[t][:], mixed_middle[:, t : t + 1], ACT.Exp, bias=partial[:], scale=SHARPNESS)
             share[t] = stat("share%d" % t, 2)
             nc.scalar.activation(share[t][:, 0:1], odds[t][:], ACT.Copy, bias=1.0)
 
@@ -171,17 +198,19 @@ def tile_picked_ydola_soft_p_kernel(tc, x_words, x_scales, hT, gT, fT, offs, out
                 blend[t][:], lead[EARLY, t][:], odds[t][:], lead[MIDDLE, t][:], ALU.mult, ALU.add
             )
             nc.vector.reciprocal(share[t][:, 1:2], share[t][:, 0:1])
-        final = {}
+        numerator, total = {}, {}
         for t in range(TILES):
             low = stat("low%d" % t, 1)
             neg_g = wide("neg_g%d" % t)
             nc.vector.tensor_scalar(neg_g[:], blend[t][:], share[t][:, 1:2], None, ALU.mult, ALU.min, accum_out=low[:])
-            final[t] = (wide("final%d" % t), stat("total%d" % t, 1))
-            nc.scalar.activation(final[t][0][:], neg_g[:], ACT.Exp, bias=low[:], scale=-1.0, accum_out=final[t][1][:])
+            numerator[t] = wide("numerator%d" % t)
+            total[t] = stat("total%d" % t, 1)
+            nc.scalar.activation(numerator[t][:], neg_g[:], ACT.Exp, bias=low[:], scale=-1.0, accum_out=total[t][:])
+        half = S // 2
         for t in range(TILES):
             inv_total = stat("inv_total%d" % t, 1)
-            nc.vector.reciprocal(inv_total[:], final[t][1][:])
-            for c in range(0, S, S // 2):
-                result = keep.tile([P, S // 2], F32, name="result%d_%d" % (t, c))
-                nc.vector.tensor_scalar(result[:], final[t][0][:, c : c + S // 2], inv_total[:], None, ALU.mult)
-                nc.sync.dma_start(out=out[t * P : (t + 1) * P, c : c + S // 2], in_=result[:])
+            nc.vector.reciprocal(inv_total[:], total[t][:])
+            for c in range(0, S, half):
+                result = keep.tile([P, half], F32, name="result%d_%d" % (t, c))
+                nc.vector.tensor_scalar(result[:], numerator[t][:, c : c + half], inv_total[:], None, ALU.mult)
+                nc.sync.dma_start(out=out[t * P : (t + 1) * P, c : c + half], in_=result[:])

from contextlib import ExitStack

import concourse.mybir as mybir

K, T, S, V = 512, 1024, 512, 256
FLOPS = 3 * 2 * K * V * S

F32 = mybir.dt.float32
BF16 = mybir.dt.bfloat16
I32 = mybir.dt.int32
U32 = mybir.dt.uint32
U16 = mybir.dt.uint16
U8 = mybir.dt.uint8
FP8X4 = mybir.dt.float8_e4m3fn_x4
ALU = mybir.AluOpType
ACT = mybir.ActivationFunctionType
AX = mybir.AxisListType

P = 128
PACK = 4
QUADRANTS = 4
TILES = V // P
LAST, EARLY, MIDDLE = 0, 1, 2
LAYERS = (LAST, EARLY, MIDDLE)
EARLIER = (EARLY, MIDDLE)
PAIRS = [(m, t) for t in range(TILES) for m in EARLIER]
FINAL_PRODUCT = (MIDDLE, TILES - 1)
SHARPNESS = 4.0
LOG_OF_FLOOR = -42.0
MIXED_EARLY = 0
LOG_SUM = {EARLY: 1, MIDDLE: 2}
OWN = {EARLY: 3, MIDDLE: 4}
TERMS = 5


def tile_picked_ydola_soft_p_kernel(tc, x_words, x_scales, hT, gT, fT, offs, out):
    nc = tc.nc
    with ExitStack() as ctx:
        keep = ctx.enter_context(tc.tile_pool(name="keep", bufs=1))
        psum = ctx.enter_context(tc.psum_pool(name="psum", bufs=1))

        def wide(name, reuse=None):
            return keep.tile([P, S], F32, name=name, tag=reuse or name, align_bytes=64)

        def stat(name, cols):
            return keep.tile([P, cols], F32, name=name)

        offsets = keep.tile([P, S // 16], U16, name="offsets")
        nc.sync.dma_start(offsets[:], offs)
        table_words = keep.tile([P, T], I32, name="table_words")
        nc.sync.dma_start(out=table_words[:], in_=x_words[0].rearrange("p n t -> p (n t)").bitcast(I32))
        table_scales = keep.tile([P, T], U8, name="table_scales")
        nc.gpsimd.memset(table_scales[:].bitcast(I32), 0)
        for quad in range(QUADRANTS):
            nc.sync.dma_start(
                out=table_scales[32 * quad : 32 * quad + 4, :].bitcast(I32),
                in_=x_scales[0][4 * quad : 4 * quad + 4, :].bitcast(I32),
            )
        raw = []
        for m, states in enumerate((hT, gT, fT)):
            raw.append(keep.tile([P, PACK, V], F32, name="raw%d" % m, tag="raw%d" % m, align_bytes=64))
            nc.sync.dma_start(out=raw[m][:], in_=states.rearrange("(p j) w -> p j w", j=PACK))

        floor_log = stat("floor_log", 1)
        nc.gpsimd.memset(floor_log[:], LOG_OF_FLOOR)
        floor = stat("floor", 1)
        nc.scalar.activation(floor[:], floor_log[:], ACT.Exp)

        x_codes = keep.tile([P, S], U32, name="x_codes", align_bytes=64)
        nc.vector.tensor_copy(x_codes[:], table_words[:].bitcast(U32).indirect(offsets[:]))
        x_sc = keep.tile([P, S], U8, name="x_sc", align_bytes=64)
        nc.vector.tensor_copy(x_sc[:], table_scales[:].indirect(offsets[:]))

        logits = {}
        for m in LAYERS:
            grouped = []
            for t in range(TILES):
                name = "grouped%d%d" % (m, t)
                grouped.append(keep.tile([P, P, PACK], BF16, name=name, tag=name, align_bytes=64))
                src = raw[m][:, :, t * P : (t + 1) * P].rearrange("p j (c i) -> p c j i", i=PACK)
                dst = grouped[t][:].rearrange("p (c i) j -> p c j i", i=PACK)
                if (m, t) == (EARLY, 0):
                    nc.vector.tensor_copy(dst, src)
                else:
                    nc.scalar.activation(dst, src, ACT.Copy)
            for t in range(TILES):
                codes = keep.tile([P, P], U32, name="codes%d%d" % (m, t), align_bytes=64)
                scales = keep.tile([P, P], U8, name="scales%d%d" % (m, t), align_bytes=64)
                nc.vector.quantize_mx(
                    out=codes[:].bitcast(FP8X4), scales=scales[:], in_=grouped[t][:].rearrange("p w j -> p (w j)")
                )
                logits[m, t] = psum.tile([P, S], F32, name="logits%d%d" % (m, t))
                nc.tensor.matmul_mx(
                    out=logits[m, t][:],
                    lhsT=codes[:].bitcast(FP8X4),
                    lhsT_scale=scales[:],
                    rhs=x_codes[:].bitcast(FP8X4),
                    rhs_scale=x_sc[:],
                    start=True,
                    stop=True,
                )

        def col(m, t):
            return slice(m * TILES + t, m * TILES + t + 1)

        def pair(m, t):
            return col(m - 1, t)

        neg_max = stat("neg_max", len(LAYERS) * TILES)
        sums = stat("sums", len(LAYERS) * TILES)
        e, neg, lead = {}, {}, {}
        for m in LAYERS:
            for t in range(TILES):
                if (m, t) == FINAL_PRODUCT:
                    nc.vector.tensor_reduce(neg_max[:, col(m, t)], logits[m, t][:], AX.X, ALU.max, negate=True)
                else:
                    neg[m, t] = wide("neg%d%d" % (m, t), "grouped%d%d" % (MIDDLE, t) if m == EARLY else None)
                    nc.vector.tensor_scalar(
                        neg[m, t][:], logits[m, t][:], -1.0, None, ALU.mult, ALU.min, accum_out=neg_max[:, col(m, t)]
                    )
                e[m, t] = wide("e%d%d" % (m, t), "raw%d" % MIDDLE if (m, t) == (LAST, 0) else None)
                nc.scalar.activation(
                    e[m, t][:], logits[m, t][:], ACT.Exp, bias=neg_max[:, col(m, t)], accum_out=sums[:, col(m, t)]
                )
                if m != LAST:
                    lead[m, t] = wide("lead%d%d" % (m, t))
                    if (m, t) == FINAL_PRODUCT:
                        nc.vector.tensor_tensor(lead[m, t][:], logits[m, t][:], neg[LAST, t][:], ALU.add)
                    else:
                        nc.gpsimd.tensor_tensor(lead[m, t][:], neg[LAST, t][:], neg[m, t][:], ALU.subtract)

        terms = keep.tile([P, TILES, TERMS], F32, name="terms")
        coef = keep.tile([P, TILES, TERMS], F32, name="coef")
        nc.gpsimd.memset(coef[:, :, MIXED_EARLY : LOG_SUM[EARLY] + 1], -SHARPNESS)
        nc.gpsimd.memset(coef[:, :, LOG_SUM[MIDDLE] : LOG_SUM[MIDDLE] + 1], SHARPNESS)
        mixed_middle = stat("mixed_middle", TILES)
        ratio = stat("ratio", len(EARLIER) * TILES)
        inv_last = stat("inv_last", TILES)
        inv = stat("inv", len(EARLIER) * TILES)

        def own_term(m, t, reuse=None):
            nc.vector.scalar_tensor_tensor(
                wide("own_terms%d%d" % (m, t), reuse)[:], logits[m, t][:], neg_max[:, col(m, t)], e[m, t][:],
                ALU.add, ALU.mult, accum_out=terms[:, t, OWN[m] : OWN[m] + 1],
            )

        nc.vector.reciprocal(inv_last[:], sums[:, 0:TILES])
        for m in EARLIER:
            for t in range(TILES):
                if (m, t) != FINAL_PRODUCT:
                    own_term(m, t)
        for t in range(TILES):
            nc.scalar.activation(
                ratio[:, t::TILES], sums[:, TILES + t :: TILES], ACT.Identity, scale=inv_last[:, t : t + 1]
            )
        nc.vector.reciprocal(inv[:], sums[:, TILES:])

        scaled_q, log_q = {}, {}
        for m, t in PAIRS:
            scaled_q[m, t] = wide("scaled_q%d%d" % (m, t))
            nc.vector.scalar_tensor_tensor(
                scaled_q[m, t][:], e[LAST, t][:], ratio[:, pair(m, t)], e[m, t][:], ALU.mult, ALU.add
            )
        own_term(MIDDLE, TILES - 1, "e%d%d" % (LAST, TILES - 1))

        nc.scalar.activation(
            terms[:, :, LOG_SUM[EARLY] : LOG_SUM[MIDDLE] + 1].rearrange("p t m -> p m t"),
            sums[:, TILES:].rearrange("p (m t) -> p m t", t=TILES),
            ACT.Ln,
        )
        for m, factor in ((EARLY, SHARPNESS), (MIDDLE, -SHARPNESS)):
            nc.scalar.activation(coef[:, :, OWN[m]], inv[:, (m - 1) * TILES : m * TILES], ACT.Copy, scale=factor)
        for m, t in PAIRS:
            log_q[m, t] = wide("log_q%d%d" % (m, t))
            nc.scalar.activation(log_q[m, t][:], scaled_q[m, t][:], ACT.Ln, bias=floor[:], scale=inv[:, pair(m, t)])

        odds, share = {}, {}
        for t in range(TILES):
            for m, mixed in ((EARLY, terms[:, t, MIXED_EARLY : MIXED_EARLY + 1]), (MIDDLE, mixed_middle[:, t : t + 1])):
                nc.vector.scalar_tensor_tensor(
                    wide("mixed_terms%d%d" % (m, t))[:], scaled_q[m, t][:], inv[:, pair(m, t)], log_q[m, t][:],
                    ALU.mult, ALU.mult, accum_out=mixed,
                )
            partial = stat("partial%d" % t, 1)
            nc.vector.scalar_tensor_tensor(
                stat("weighted%d" % t, TERMS)[:], terms[:, t, :], 1.0, coef[:, t, :],
                ALU.mult, ALU.mult, accum_out=partial[:],
            )
            odds[t] = stat("odds%d" % t, 1)
            nc.scalar.activation(odds[t][:], mixed_middle[:, t : t + 1], ACT.Exp, bias=partial[:], scale=SHARPNESS)
            share[t] = stat("share%d" % t, 2)
            nc.scalar.activation(share[t][:, 0:1], odds[t][:], ACT.Copy, bias=1.0)

        blend = {}
        for t in range(TILES):
            blend[t] = wide("blend%d" % t)
            nc.vector.scalar_tensor_tensor(
                blend[t][:], lead[EARLY, t][:], odds[t][:], lead[MIDDLE, t][:], ALU.mult, ALU.add
            )
            nc.vector.reciprocal(share[t][:, 1:2], share[t][:, 0:1])
        numerator, total = {}, {}
        for t in range(TILES):
            low = stat("low%d" % t, 1)
            neg_g = wide("neg_g%d" % t)
            nc.vector.tensor_scalar(neg_g[:], blend[t][:], share[t][:, 1:2], None, ALU.mult, ALU.min, accum_out=low[:])
            numerator[t] = wide("numerator%d" % t)
            total[t] = stat("total%d" % t, 1)
            nc.scalar.activation(numerator[t][:], neg_g[:], ACT.Exp, bias=low[:], scale=-1.0, accum_out=total[t][:])
        half = S // 2
        for t in range(TILES):
            inv_total = stat("inv_total%d" % t, 1)
            nc.vector.reciprocal(inv_total[:], total[t][:])
            for c in range(0, S, half):
                result = keep.tile([P, half], F32, name="result%d_%d" % (t, c))
                nc.vector.tensor_scalar(result[:], numerator[t][:, c : c + half], inv_total[:], None, ALU.mult)
                nc.sync.dma_start(out=out[t * P : (t + 1) * P, c : c + half], in_=result[:])
